import numpy as np
import ml_dtypes


def mxq(x, axis, fmt="e4m3"):
    dtype, down = {"e4m3": (ml_dtypes.float8_e4m3fn, 7), "e5m2": (ml_dtypes.float8_e5m2, 14)}[fmt]
    v = np.moveaxis(np.asarray(x, np.float32).astype(ml_dtypes.bfloat16).astype(np.float64), axis, -1)
    blocks = v.reshape(v.shape[:-1] + (-1, 32))
    amax = np.abs(blocks).max(-1, keepdims=True)
    byte = np.maximum(np.where(amax > 0, np.frexp(amax)[1] - 1 + 127, 0) - down, 1)
    scale = np.exp2(byte - 127.0)
    codes = (blocks / scale).astype(np.float32).astype(dtype).astype(np.float64)
    return np.moveaxis((codes * scale).reshape(v.shape), -1, axis)


WIDE = False


def mx_kscale(k):
    if not WIDE:
        return np.ones(k)
    levels = np.array([10, -10, 5, -5, 0])
    if k % 512:
        return np.exp2(np.random.permutation(np.resize(levels, k // 32))).repeat(32)
    a = np.empty((k // 512, 16))
    for p in range(k // 512):
        a[p, :8] = np.random.permutation(np.resize(levels, 8))
        for g in range(8):
            far = levels[np.abs(levels - a[p, g]) >= 10]
            a[p, g + 8] = far[np.random.randint(len(far))]
    return np.exp2(a.ravel()).repeat(32)


def f64(x):
    return np.asarray(x).astype(np.float64)


def striped(idx):
    return np.tile(idx.reshape(-1, 16).T, (8, 1)).astype(np.uint16)


def unstriped(offs):
    return offs[:16].T.reshape(-1).astype(np.int64)


def pack_weight(w):
    k, n = w.shape
    w = f64(np.asarray(w, np.float32).astype(ml_dtypes.bfloat16)).reshape(k // 32, 32, n)
    amax = np.abs(w).max(1)
    byte = np.clip(np.where(amax > 0, np.frexp(amax)[1] - 1 + 127 - 7, 1), 1, 254)
    scaled = (w * np.exp2(127.0 - byte)[:, None, :]).reshape(k, n).astype(np.float32)
    words = np.ascontiguousarray(scaled.reshape(k // 512, 128, 4, n).transpose(0, 1, 3, 2)).astype(ml_dtypes.float8_e4m3fn).view(np.uint8)
    return words, np.ascontiguousarray(byte.astype(np.uint8).reshape(k // 512, 16, n))


def unpack_weight(words, scales):
    g, p, n, _ = words.shape
    vals = np.ascontiguousarray(words).view(ml_dtypes.float8_e4m3fn).astype(np.float64) * np.repeat(np.exp2(scales.astype(np.float64) - 127.0), 8, axis=1)[..., None]
    return vals.transpose(0, 1, 3, 2).reshape(g * 512, n)


K, T, S, N, U, V = 1024, 1024, 512, 256, 512, 256
P = 2 ** 7


def setup_inputs():
    n = np.random.standard_normal
    s = mx_kscale(K)[:, None]
    packed_xT = pack_weight(n((K, T)) * s)
    return {
        "x_words": packed_xT[0],
        "x_scales": packed_xT[1],
        "w1": (n((K, N)) / np.sqrt(K) / s).astype(np.float32),
        "im": (np.tile(np.random.uniform(0.2, 1.5, S), (P, 1))).astype(np.float32),
        "lam": (np.tile(n(U) * 0.3, (P, 1))).astype(np.float32),
        "comp": (np.tile(np.random.uniform(0.05, 0.6, U), (P, 1))).astype(np.float32),
        "rest": (np.tile(np.random.uniform(0.3, 1.2, U), (P, 1))).astype(np.float32),
        "offs": striped(np.random.permutation(T)[:S]),
        "pa": striped(np.random.randint(0, S, U)),
        "pb": striped(np.random.randint(0, S, U)),
        "inc1": striped(np.random.permutation(U)[:V]),
        "inc2": striped(np.random.permutation(U)[:V]),
        "who": striped(np.random.permutation(S)[:V]),
    }


def reference(x_words, x_scales, w1, im, lam, comp, rest, offs, pa, pb, inc1, inc2, who):
    xq = unpack_weight(x_words, x_scales)[:, unstriped(offs)]
    y = mxq(f64(w1), 0, "e4m3").T @ xq
    df = y[:, unstriped(pa)] - y[:, unstriped(pb)]
    ln = np.sqrt((df) ** 2 + 0.02)
    cons = ln - f64(rest)[:1]
    dl = (-1.0 * (cons + f64(comp)[:1] * f64(lam)[:1])) / (f64(im)[:1][:, unstriped(pa)] + f64(im)[:1][:, unstriped(pb)] + f64(comp)[:1])
    push = (dl * df) / ln
    return y[:, unstriped(who)] + (f64(im)[:1][:, unstriped(who)]) * (push[:, unstriped(inc1)] - push[:, unstriped(inc2)])

@@ -1,0 +1,207 @@
+from contextlib import ExitStack
+
+import concourse.mybir as mybir
+from concourse.masks import make_identity
+
+K, T, S, N, U, V = 1024, 1024, 512, 256, 512, 256
+FLOPS = 2 * K * S * N
+
+F32 = mybir.dt.float32
+BF16 = mybir.dt.bfloat16
+I32 = mybir.dt.int32
+U32 = mybir.dt.uint32
+U16 = mybir.dt.uint16
+U8 = mybir.dt.uint8
+FP8X4 = mybir.dt.float8_e4m3fn_x4
+ALU = mybir.AluOpType
+ACT = mybir.ActivationFunctionType
+
+P = 128
+PACK = 4
+K_PASS = P * PACK
+PASSES = K // K_PASS
+TILES = N // P
+HALF = U // 2
+BLOCKS = U // P
+EPS = 0.02
+WIDE = 704
+
+
+def tile_picked_yxpbd_pos_p_kernel(tc, x_words, x_scales, w1, im, lam, comp, rest, offs, pa, pb, inc1, inc2, who, out):
+    nc = tc.nc
+    with ExitStack() as ctx:
+        sb = ctx.enter_context(tc.tile_pool(name="sb", bufs=1))
+        ps = ctx.enter_context(tc.psum_pool(name="ps", bufs=1))
+
+        def tile(shape, dtype, name, tag=None):
+            return sb.tile(shape, dtype, name=name, tag=tag or name, align_bytes=64)
+
+        def load_list(src, name):
+            t = tile(list(src.shape), U16, name)
+            nc.sync.dma_start(t[:], src)
+            return t
+
+        def half(lst, h):
+            return lst[:, h * (HALF // 16) : (h + 1) * (HALF // 16)]
+
+        def tr(dst, src, first, last):
+            nc.tensor.matmul(dst, lhsT=src, rhs=ident[:], is_transpose=True, start=first, stop=last)
+
+        xs = tile([P, T], U8, "xs")
+        nc.gpsimd.memset(xs[:].bitcast(I32), 0)
+        rows = tile([P, P], F32, "rows")
+        nc.gpsimd.memset(rows[:], 0.0)
+        ident = tile([P, P], F32, "ident")
+        make_identity(nc, ident[:])
+        warm = tile([P, 1], F32, "warm")
+        nc.scalar.activation(warm[:], rows[:, 0:1], ACT.Abs_reciprocal_sqrt, bias=EPS)
+
+        pa_t = load_list(pa, "pa_t")
+        im_t = tile([P, WIDE], F32, "im_t")
+        nc.gpsimd.memset(im_t[:, S:WIDE], 0.0)
+        nc.sync.dma_start(im_t[:, 0:S], im)
+        offs_t = load_list(offs, "offs_t")
+        xw = [tile([P, T], U32, f"xw{o}") for o in range(PASSES)]
+        w_raw = [tile([P, PACK, N], F32, f"w_raw{o}") for o in range(PASSES)]
+
+        def load_x(o):
+            nc.sync.dma_start(xw[o][:].bitcast(I32), x_words[o].rearrange("p c r -> p (c r)").bitcast(I32))
+
+        def load_w(o):
+            nc.sync.dma_start(w_raw[o][:], w1[o * K_PASS : (o + 1) * K_PASS, :].rearrange("(p j) n -> p j n", j=PACK))
+
+        load_x(0)
+        for q in range(4):
+            nc.sync.dma_start(xs[32 * q : 32 * q + 8, :].bitcast(I32), x_scales[:, 4 * q : 4 * q + 4, :].bitcast(I32))
+        load_w(0)
+        load_w(1)
+        load_x(1)
+        pb_t = load_list(pb, "pb_t")
+        for i, src in enumerate((comp, lam, rest)):
+            nc.gpsimd.dma_start(rows[4 * i : 4 * i + 4, :], src[0].rearrange("(c p) -> c p", p=P))
+        who_t = load_list(who, "who_t")
+        inc1_t = load_list(inc1, "inc1_t")
+        inc2_t = load_list(inc2, "inc2_t")
+
+        ima = tile([P, U], F32, "ima")
+        imb = tile([P, U], F32, "imb")
+        nc.vector.tensor_copy(ima[:], im_t[:].indirect(pa_t[:]))
+
+        gw = [tile([P, S], U32, f"gw{o}") for o in range(PASSES)]
+        gs = tile([P, S], U8, "gs")
+        wq = {}
+        ws = {}
+
+        def quant(o):
+            wb = tile([P, N, PACK], BF16, f"wb{o}")
+            nc.scalar.copy(wb[:], w_raw[o][:].rearrange("p j m -> p m j"))
+            wq[o] = tile([P, N], U32, f"wq{o}")
+            ws[o] = tile([P, N], U8, f"ws{o}")
+            nc.vector.quantize_mx(out=wq[o][:].bitcast(FP8X4), scales=ws[o][:], in_=wb[:].rearrange("p m j -> p (m j)"))
+
+        nc.vector.tensor_copy(gw[0][:], xw[0][:].indirect(offs_t[:]))
+        nc.vector.tensor_copy(gs[:], xs[:].indirect(offs_t[:]))
+        for o in range(PASSES):
+            quant(o)
+        nc.vector.tensor_copy(gw[1][:], xw[1][:].indirect(offs_t[:]))
+
+        y = [tile([P, S], F32, f"y{t}") for t in range(TILES)]
+        yn = [tile([P, S], F32, f"yn{t}") for t in range(TILES)]
+        for t in range(TILES):
+            acc = ps.tile([P, S], F32, name=f"acc{t}")
+            for o in range(PASSES):
+                nc.tensor.matmul_mx(out=acc[:], lhsT=wq[o][:, t * P : (t + 1) * P].bitcast(FP8X4), lhsT_scale=ws[o][:, t * P : (t + 1) * P],
+                                    rhs=gw[o][:].bitcast(FP8X4), rhs_scale=gs[4 * o : P, :],
+                                    start=(o == 0), stop=(o == PASSES - 1))
+            nc.scalar.copy(y[t][:], acc[:])
+            nc.scalar.activation(yn[t][:], acc[:], ACT.Copy, scale=-1.0)
+
+        nc.vector.tensor_copy(imb[:], im_t[:].indirect(pb_t[:]))
+        imw = tile([P, V], F32, "imw")
+        nc.vector.tensor_copy(imw[:], im_t[:].indirect(who_t[:]))
+
+        par_ps = ps.tile([P, P], F32, name="par_ps")
+        tr(par_ps[:], rows[:], True, True)
+        par = tile([P, 3 * BLOCKS], F32, "par")
+        nc.scalar.copy(par[:], par_ps[:, 0 : 3 * BLOCKS])
+        cl = tile([P, BLOCKS], F32, "cl")
+        nc.gpsimd.tensor_tensor(cl[:], par[:, 0:4], par[:, 4:8], ALU.mult)
+        nc0 = tile([P, BLOCKS], F32, "nc0", tag="ga00")
+        nc.gpsimd.tensor_tensor(nc0[:], cl[:], par[:, 8:12], ALU.subtract)
+        den_ps = ps.tile([P, BLOCKS, P], F32, name="den_ps")
+        for c in range(BLOCKS):
+            cols = slice(c * P, (c + 1) * P)
+            tr(den_ps[:, c, :], ima[:, cols], True, False)
+            tr(den_ps[:, c, :], imb[:, cols], False, True)
+        nden = tile([P, BLOCKS], F32, "nden")
+        nc.vector.scalar_tensor_tensor(nden[:], den_ps[:, :, 0], -1.0, par[:, 0:4], ALU.mult, ALU.subtract)
+        nb = tile([P, BLOCKS], F32, "nb")
+        nc.vector.reciprocal(nb[:], nden[:])
+        aa = tile([P, BLOCKS], F32, "aa")
+        nc.vector.tensor_tensor(aa[:], nc0[:], nb[:], ALU.mult)
+
+        push = [tile([P, U], F32, f"push{t}") for t in range(TILES)]
+        df_ps = {}
+        gain = {}
+
+        def front(t, h):
+            ga = tile([P, HALF], F32, f"ga{t}{h}", tag="g00" if (t, h) == (1, 1) else None)
+            gb = tile([P, HALF], F32, f"gb{t}{h}")
+            nc.vector.tensor_copy(ga[:], y[t][:].indirect(half(pa_t, h)))
+            nc.vector.tensor_copy(gb[:], yn[t][:].indirect(half(pb_t, h)))
+            d = ps.tile([P, 2, P], F32, name=f"df{t}{h}", tag=f"bank{t}{h}")
+            for b in range(2):
+                tr(d[:, b, :], ga[:, b * P : (b + 1) * P], True, False)
+                tr(d[:, b, :], gb[:, b * P : (b + 1) * P], False, True)
+            sq = tile([P, 2, P], F32, f"sq{t}{h}")
+            nc.scalar.activation(sq[:], d[:], ACT.Square)
+            rl = tile([P, 2, P], F32, f"rl{t}{h}")
+            nc.scalar.activation(rl[:], sq[:], ACT.Abs_reciprocal_sqrt, bias=EPS)
+            g = tile([P, 2, P], F32, f"g{t}{h}")
+            for b in range(2):
+                c = 2 * h + b
+                nc.scalar.activation(g[:, b, :], rl[:, b, :], ACT.Identity, bias=nb[:, c : c + 1], scale=aa[:, c : c + 1])
+            df_ps[t, h] = d
+            gain[t, h] = g
+
+        def back(t, h):
+            pt = tile([P, 2, P], F32, f"pt{t}{h}", tag={(1, 1): "g10", (0, 1): "yn1"}.get((t, h)))
+            nc.vector.tensor_tensor(pt[:], df_ps[t, h][:], gain[t, h][:], ALU.mult)
+            pp = ps.tile([P, 2, P], F32, name=f"pp{t}{h}", tag=f"bank{t}{h}")
+            for b in range(2):
+                tr(pp[:, b, :], pt[:, b, :], True, True)
+            nc.scalar.copy(push[t][:, h * HALF : (h + 1) * HALF], pp[:].rearrange("p b m -> p (b m)"))
+
+        def tail_a(t):
+            g1 = tile([P, V], F32, f"g1_{t}", tag="g10" if t == 0 else None)
+            nc.vector.tensor_copy(g1[:], push[t][:].indirect(inc1_t[:]))
+            d = tile([P, V], F32, f"d{t}")
+            nc.vector.tensor_tensor(d[:], push[t][:].indirect(inc2_t[:]), g1[:], ALU.subtract)
+            return d
+
+        def tail_b(t, d, yw):
+            e = tile([P, V], F32, f"e{t}", tag="g11" if t == 0 else None)
+            nc.vector.tensor_tensor(e[:], d[:], imw[:], ALU.mult)
+            res = tile([P, V], F32, f"res{t}")
+            nc.vector.tensor_tensor(res[:], yw[:], e[:], ALU.subtract)
+            nc.sync.dma_start(out[t * P : (t + 1) * P, :], res[:])
+
+        def fetch_who(t, tag):
+            yw = tile([P, V], F32, f"yw{t}", tag=tag)
+            nc.vector.tensor_copy(yw[:], y[t][:].indirect(who_t[:]))
+            return yw
+
+        front(0, 0)
+        front(0, 1)
+        front(1, 0)
+        back(0, 0)
+        front(1, 1)
+        back(0, 1)
+        yw0 = fetch_who(0, "g01")
+        back(1, 0)
+        d0 = tail_a(0)
+        back(1, 1)
+        tail_b(0, d0, yw0)
+        yw1 = fetch_who(1, "g11")
+        d1 = tail_a(1)
+        tail_b(1, d1, yw1)

@@ -51,14 +51,16 @@ def tile_picked_yxpbd_pos_p_kernel(tc, x_words, x_scales, w1, im, lam, comp, res
         nc.gpsimd.memset(xs[:].bitcast(I32), 0)
         rows = tile([P, P], F32, "rows")
         nc.gpsimd.memset(rows[:], 0.0)
+        im_t = tile([P, WIDE], F32, "im_t")
+        nc.gpsimd.memset(im_t[:, S:WIDE], 0.0)
+        for i, src in enumerate((comp, lam, rest)):
+            nc.gpsimd.dma_start(rows[4 * i : 4 * i + 4, :], src[0].rearrange("(c p) -> c p", p=P))
         ident = tile([P, P], F32, "ident")
         make_identity(nc, ident[:])
         warm = tile([P, 1], F32, "warm")
-        nc.scalar.activation(warm[:], rows[:, 0:1], ACT.Abs_reciprocal_sqrt, bias=EPS)
+        nc.scalar.activation(warm[:], im_t[:, S : S + 1], ACT.Abs_reciprocal_sqrt, bias=EPS)
 
         pa_t = load_list(pa, "pa_t")
-        im_t = tile([P, WIDE], F32, "im_t")
-        nc.gpsimd.memset(im_t[:, S:WIDE], 0.0)
         nc.sync.dma_start(im_t[:, 0:S], im)
         offs_t = load_list(offs, "offs_t")
         xw = [tile([P, T], U32, f"xw{o}") for o in range(PASSES)]
@@ -77,8 +79,6 @@ def tile_picked_yxpbd_pos_p_kernel(tc, x_words, x_scales, w1, im, lam, comp, res
         load_w(1)
         load_x(1)
         pb_t = load_list(pb, "pb_t")
-        for i, src in enumerate((comp, lam, rest)):
-            nc.gpsimd.dma_start(rows[4 * i : 4 * i + 4, :], src[0].rearrange("(c p) -> c p", p=P))
         who_t = load_list(who, "who_t")
         inc1_t = load_list(inc1, "inc1_t")
         inc2_t = load_list(inc2, "inc2_t")
@@ -87,6 +87,14 @@ def tile_picked_yxpbd_pos_p_kernel(tc, x_words, x_scales, w1, im, lam, comp, res
         imb = tile([P, U], F32, "imb")
         nc.vector.tensor_copy(ima[:], im_t[:].indirect(pa_t[:]))
 
+        par_ps = ps.tile([P, P], F32, name="par_ps")
+        tr(par_ps[:], rows[:], True, True)
+        par = tile([P, 3 * BLOCKS], F32, "par")
+        nc.scalar.copy(par[:], par_ps[:, 0 : 3 * BLOCKS])
+        cl = tile([P, BLOCKS], F32, "cl")
+        nc.gpsimd.tensor_tensor(cl[:], par[:, 0:4], par[:, 4:8], ALU.mult)
+        nc0 = tile([P, BLOCKS], F32, "nc0", tag="ga01")
+        nc.gpsimd.tensor_tensor(nc0[:], cl[:], par[:, 8:12], ALU.subtract)
         gw = [tile([P, S], U32, f"gw{o}") for o in range(PASSES)]
         gs = tile([P, S], U8, "gs")
         wq = {}
@@ -120,14 +128,6 @@ def tile_picked_yxpbd_pos_p_kernel(tc, x_words, x_scales, w1, im, lam, comp, res
         imw = tile([P, V], F32, "imw")
         nc.vector.tensor_copy(imw[:], im_t[:].indirect(who_t[:]))
 
-        par_ps = ps.tile([P, P], F32, name="par_ps")
-        tr(par_ps[:], rows[:], True, True)
-        par = tile([P, 3 * BLOCKS], F32, "par")
-        nc.scalar.copy(par[:], par_ps[:, 0 : 3 * BLOCKS])
-        cl = tile([P, BLOCKS], F32, "cl")
-        nc.gpsimd.tensor_tensor(cl[:], par[:, 0:4], par[:, 4:8], ALU.mult)
-        nc0 = tile([P, BLOCKS], F32, "nc0", tag="ga00")
-        nc.gpsimd.tensor_tensor(nc0[:], cl[:], par[:, 8:12], ALU.subtract)
         den_ps = ps.tile([P, BLOCKS, P], F32, name="den_ps")
         for c in range(BLOCKS):
             cols = slice(c * P, (c + 1) * P)
@@ -165,31 +165,37 @@ def tile_picked_yxpbd_pos_p_kernel(tc, x_words, x_scales, w1, im, lam, comp, res
             gain[t, h] = g
 
         def back(t, h):
-            pt = tile([P, 2, P], F32, f"pt{t}{h}", tag={(1, 1): "g10", (0, 1): "yn1"}.get((t, h)))
+            pt = tile([P, 2, P], F32, f"pt{t}{h}", tag={(0, 1): "yn1"}.get((t, h)))
             nc.vector.tensor_tensor(pt[:], df_ps[t, h][:], gain[t, h][:], ALU.mult)
             pp = ps.tile([P, 2, P], F32, name=f"pp{t}{h}", tag=f"bank{t}{h}")
             for b in range(2):
                 tr(pp[:, b, :], pt[:, b, :], True, True)
             nc.scalar.copy(push[t][:, h * HALF : (h + 1) * HALF], pp[:].rearrange("p b m -> p (b m)"))
 
-        def tail_a(t):
-            g1 = tile([P, V], F32, f"g1_{t}", tag="g10" if t == 0 else None)
-            nc.vector.tensor_copy(g1[:], push[t][:].indirect(inc1_t[:]))
-            d = tile([P, V], F32, f"d{t}")
-            nc.vector.tensor_tensor(d[:], push[t][:].indirect(inc2_t[:]), g1[:], ALU.subtract)
-            return d
-
-        def tail_b(t, d, yw):
-            e = tile([P, V], F32, f"e{t}", tag="g11" if t == 0 else None)
-            nc.vector.tensor_tensor(e[:], d[:], imw[:], ALU.mult)
-            res = tile([P, V], F32, f"res{t}")
-            nc.vector.tensor_tensor(res[:], yw[:], e[:], ALU.subtract)
-            nc.sync.dma_start(out[t * P : (t + 1) * P, :], res[:])
-
         def fetch_who(t, tag):
             yw = tile([P, V], F32, f"yw{t}", tag=tag)
             nc.vector.tensor_copy(yw[:], y[t][:].indirect(who_t[:]))
             return yw
+
+        def plus(t):
+            g1 = tile([P, V], F32, f"g1_{t}", tag="g11")
+            nc.vector.tensor_copy(g1[:], push[t][:].indirect(inc1_t[:]))
+            return g1
+
+        def minus(t, g1, tag):
+            d = tile([P, V], F32, f"d{t}", tag=tag)
+            nc.vector.tensor_tensor(d[:], push[t][:].indirect(inc2_t[:]), g1[:], ALU.subtract)
+            return d
+
+        def weigh(t, d):
+            e = tile([P, V], F32, f"e{t}")
+            nc.vector.tensor_tensor(e[:], d[:], imw[:], ALU.mult)
+            return e
+
+        def finish(t, yw, e):
+            res = tile([P, V], F32, f"res{t}")
+            nc.vector.tensor_tensor(res[:], yw[:], e[:], ALU.subtract)
+            nc.sync.dma_start(out[t * P : (t + 1) * P, :], res[:])
 
         front(0, 0)
         front(0, 1)
@@ -199,9 +205,13 @@ def tile_picked_yxpbd_pos_p_kernel(tc, x_words, x_scales, w1, im, lam, comp, res
         back(0, 1)
         yw0 = fetch_who(0, "g01")
         back(1, 0)
-        d0 = tail_a(0)
+        yw1 = fetch_who(1, "g10")
         back(1, 1)
-        tail_b(0, d0, yw0)
-        yw1 = fetch_who(1, "g11")
-        d1 = tail_a(1)
-        tail_b(1, d1, yw1)
+        p0 = plus(0)
+        d0 = minus(0, p0, "pt11")
+        p1 = plus(1)
+        e0 = weigh(0, d0)
+        d1 = minus(1, p1, None)
+        finish(0, yw0, e0)
+        e1 = weigh(1, d1)
+        finish(1, yw1, e1)

from contextlib import ExitStack

import concourse.mybir as mybir
from concourse.masks import make_identity

K, T, S, N, U, V = 1024, 1024, 512, 256, 512, 256
FLOPS = 2 * K * S * N

F32 = mybir.dt.float32
BF16 = mybir.dt.bfloat16
I32 = mybir.dt.int32
U32 = mybir.dt.uint32
U16 = mybir.dt.uint16
U8 = mybir.dt.uint8
FP8X4 = mybir.dt.float8_e4m3fn_x4
ALU = mybir.AluOpType
ACT = mybir.ActivationFunctionType

P = 128
PACK = 4
K_PASS = P * PACK
PASSES = K // K_PASS
TILES = N // P
HALF = U // 2
BLOCKS = U // P
EPS = 0.02
WIDE = 704


def tile_picked_yxpbd_pos_p_kernel(tc, x_words, x_scales, w1, im, lam, comp, rest, offs, pa, pb, inc1, inc2, who, out):
    nc = tc.nc
    with ExitStack() as ctx:
        sb = ctx.enter_context(tc.tile_pool(name="sb", bufs=1))
        ps = ctx.enter_context(tc.psum_pool(name="ps", bufs=1))

        def tile(shape, dtype, name, tag=None):
            return sb.tile(shape, dtype, name=name, tag=tag or name, align_bytes=64)

        def load_list(src, name):
            t = tile(list(src.shape), U16, name)
            nc.sync.dma_start(t[:], src)
            return t

        def half(lst, h):
            return lst[:, h * (HALF // 16) : (h + 1) * (HALF // 16)]

        def tr(dst, src, first, last):
            nc.tensor.matmul(dst, lhsT=src, rhs=ident[:], is_transpose=True, start=first, stop=last)

        xs = tile([P, T], U8, "xs")
        nc.gpsimd.memset(xs[:].bitcast(I32), 0)
        rows = tile([P, P], F32, "rows")
        nc.gpsimd.memset(rows[:], 0.0)
        im_t = tile([P, WIDE], F32, "im_t")
        nc.gpsimd.memset(im_t[:, S:WIDE], 0.0)
        for i, src in enumerate((comp, lam, rest)):
            nc.gpsimd.dma_start(rows[4 * i : 4 * i + 4, :], src[0].rearrange("(c p) -> c p", p=P))
        ident = tile([P, P], F32, "ident")
        make_identity(nc, ident[:])
        warm = tile([P, 1], F32, "warm")
        nc.scalar.activation(warm[:], im_t[:, S : S + 1], ACT.Abs_reciprocal_sqrt, bias=EPS)

        pa_t = load_list(pa, "pa_t")
        nc.sync.dma_start(im_t[:, 0:S], im)
        offs_t = load_list(offs, "offs_t")
        xw = [tile([P, T], U32, f"xw{o}") for o in range(PASSES)]
        w_raw = [tile([P, PACK, N], F32, f"w_raw{o}") for o in range(PASSES)]

        def load_x(o):
            nc.sync.dma_start(xw[o][:].bitcast(I32), x_words[o].rearrange("p c r -> p (c r)").bitcast(I32))

        def load_w(o):
            nc.sync.dma_start(w_raw[o][:], w1[o * K_PASS : (o + 1) * K_PASS, :].rearrange("(p j) n -> p j n", j=PACK))

        load_x(0)
        for q in range(4):
            nc.sync.dma_start(xs[32 * q : 32 * q + 8, :].bitcast(I32), x_scales[:, 4 * q : 4 * q + 4, :].bitcast(I32))
        load_w(0)
        load_w(1)
        load_x(1)
        pb_t = load_list(pb, "pb_t")
        who_t = load_list(who, "who_t")
        inc1_t = load_list(inc1, "inc1_t")
        inc2_t = load_list(inc2, "inc2_t")

        ima = tile([P, U], F32, "ima")
        imb = tile([P, U], F32, "imb")
        nc.vector.tensor_copy(ima[:], im_t[:].indirect(pa_t[:]))

        par_ps = ps.tile([P, P], F32, name="par_ps")
        tr(par_ps[:], rows[:], True, True)
        par = tile([P, 3 * BLOCKS], F32, "par")
        nc.scalar.copy(par[:], par_ps[:, 0 : 3 * BLOCKS])
        cl = tile([P, BLOCKS], F32, "cl")
        nc.gpsimd.tensor_tensor(cl[:], par[:, 0:4], par[:, 4:8], ALU.mult)
        nc0 = tile([P, BLOCKS], F32, "nc0", tag="ga01")
        nc.gpsimd.tensor_tensor(nc0[:], cl[:], par[:, 8:12], ALU.subtract)
        gw = [tile([P, S], U32, f"gw{o}") for o in range(PASSES)]
        gs = tile([P, S], U8, "gs")
        wq = {}
        ws = {}

        def quant(o):
            wb = tile([P, N, PACK], BF16, f"wb{o}")
            nc.scalar.copy(wb[:], w_raw[o][:].rearrange("p j m -> p m j"))
            wq[o] = tile([P, N], U32, f"wq{o}")
            ws[o] = tile([P, N], U8, f"ws{o}")
            nc.vector.quantize_mx(out=wq[o][:].bitcast(FP8X4), scales=ws[o][:], in_=wb[:].rearrange("p m j -> p (m j)"))

        nc.vector.tensor_copy(gw[0][:], xw[0][:].indirect(offs_t[:]))
        nc.vector.tensor_copy(gs[:], xs[:].indirect(offs_t[:]))
        for o in range(PASSES):
            quant(o)
        nc.vector.tensor_copy(gw[1][:], xw[1][:].indirect(offs_t[:]))

        y = [tile([P, S], F32, f"y{t}") for t in range(TILES)]
        yn = [tile([P, S], F32, f"yn{t}") for t in range(TILES)]
        for t in range(TILES):
            acc = ps.tile([P, S], F32, name=f"acc{t}")
            for o in range(PASSES):
                nc.tensor.matmul_mx(out=acc[:], lhsT=wq[o][:, t * P : (t + 1) * P].bitcast(FP8X4), lhsT_scale=ws[o][:, t * P : (t + 1) * P],
                                    rhs=gw[o][:].bitcast(FP8X4), rhs_scale=gs[4 * o : P, :],
                                    start=(o == 0), stop=(o == PASSES - 1))
            nc.scalar.copy(y[t][:], acc[:])
            nc.scalar.activation(yn[t][:], acc[:], ACT.Copy, scale=-1.0)

        nc.vector.tensor_copy(imb[:], im_t[:].indirect(pb_t[:]))
        imw = tile([P, V], F32, "imw")
        nc.vector.tensor_copy(imw[:], im_t[:].indirect(who_t[:]))

        den_ps = ps.tile([P, BLOCKS, P], F32, name="den_ps")
        for c in range(BLOCKS):
            cols = slice(c * P, (c + 1) * P)
            tr(den_ps[:, c, :], ima[:, cols], True, False)
            tr(den_ps[:, c, :], imb[:, cols], False, True)
        nden = tile([P, BLOCKS], F32, "nden")
        nc.vector.scalar_tensor_tensor(nden[:], den_ps[:, :, 0], -1.0, par[:, 0:4], ALU.mult, ALU.subtract)
        nb = tile([P, BLOCKS], F32, "nb")
        nc.vector.reciprocal(nb[:], nden[:])
        aa = tile([P, BLOCKS], F32, "aa")
        nc.vector.tensor_tensor(aa[:], nc0[:], nb[:], ALU.mult)

        push = [tile([P, U], F32, f"push{t}") for t in range(TILES)]
        df_ps = {}
        gain = {}

        def front(t, h):
            ga = tile([P, HALF], F32, f"ga{t}{h}", tag="g00" if (t, h) == (1, 1) else None)
            gb = tile([P, HALF], F32, f"gb{t}{h}")
            nc.vector.tensor_copy(ga[:], y[t][:].indirect(half(pa_t, h)))
            nc.vector.tensor_copy(gb[:], yn[t][:].indirect(half(pb_t, h)))
            d = ps.tile([P, 2, P], F32, name=f"df{t}{h}", tag=f"bank{t}{h}")
            for b in range(2):
                tr(d[:, b, :], ga[:, b * P : (b + 1) * P], True, False)
                tr(d[:, b, :], gb[:, b * P : (b + 1) * P], False, True)
            sq = tile([P, 2, P], F32, f"sq{t}{h}")
            nc.scalar.activation(sq[:], d[:], ACT.Square)
            rl = tile([P, 2, P], F32, f"rl{t}{h}")
            nc.scalar.activation(rl[:], sq[:], ACT.Abs_reciprocal_sqrt, bias=EPS)
            g = tile([P, 2, P], F32, f"g{t}{h}")
            for b in range(2):
                c = 2 * h + b
                nc.scalar.activation(g[:, b, :], rl[:, b, :], ACT.Identity, bias=nb[:, c : c + 1], scale=aa[:, c : c + 1])
            df_ps[t, h] = d
            gain[t, h] = g

        def back(t, h):
            pt = tile([P, 2, P], F32, f"pt{t}{h}", tag={(0, 1): "yn1"}.get((t, h)))
            nc.vector.tensor_tensor(pt[:], df_ps[t, h][:], gain[t, h][:], ALU.mult)
            pp = ps.tile([P, 2, P], F32, name=f"pp{t}{h}", tag=f"bank{t}{h}")
            for b in range(2):
                tr(pp[:, b, :], pt[:, b, :], True, True)
            nc.scalar.copy(push[t][:, h * HALF : (h + 1) * HALF], pp[:].rearrange("p b m -> p (b m)"))

        def fetch_who(t, tag):
            yw = tile([P, V], F32, f"yw{t}", tag=tag)
            nc.vector.tensor_copy(yw[:], y[t][:].indirect(who_t[:]))
            return yw

        def plus(t):
            g1 = tile([P, V], F32, f"g1_{t}", tag="g11")
            nc.vector.tensor_copy(g1[:], push[t][:].indirect(inc1_t[:]))
            return g1

        def minus(t, g1, tag):
            d = tile([P, V], F32, f"d{t}", tag=tag)
            nc.vector.tensor_tensor(d[:], push[t][:].indirect(inc2_t[:]), g1[:], ALU.subtract)
            return d

        def weigh(t, d):
            e = tile([P, V], F32, f"e{t}")
            nc.vector.tensor_tensor(e[:], d[:], imw[:], ALU.mult)
            return e

        def finish(t, yw, e):
            res = tile([P, V], F32, f"res{t}")
            nc.vector.tensor_tensor(res[:], yw[:], e[:], ALU.subtract)
            nc.sync.dma_start(out[t * P : (t + 1) * P, :], res[:])

        front(0, 0)
        front(0, 1)
        front(1, 0)
        back(0, 0)
        front(1, 1)
        back(0, 1)
        yw0 = fetch_who(0, "g01")
        back(1, 0)
        yw1 = fetch_who(1, "g10")
        back(1, 1)
        p0 = plus(0)
        d0 = minus(0, p0, "pt11")
        p1 = plus(1)
        e0 = weigh(0, d0)
        d1 = minus(1, p1, None)
        finish(0, yw0, e0)
        e1 = weigh(1, d1)
        finish(1, yw1, e1)
